import numpy as np
import ml_dtypes


def mxq(x, axis, fmt="e4m3"):
    dtype, down = {"e4m3": (ml_dtypes.float8_e4m3fn, 7), "e5m2": (ml_dtypes.float8_e5m2, 14)}[fmt]
    v = np.moveaxis(np.asarray(x, np.float32).astype(ml_dtypes.bfloat16).astype(np.float64), axis, -1)
    blocks = v.reshape(v.shape[:-1] + (-1, 32))
    amax = np.abs(blocks).max(-1, keepdims=True)
    byte = np.maximum(np.where(amax > 0, np.frexp(amax)[1] - 1 + 127, 0) - down, 1)
    scale = np.exp2(byte - 127.0)
    codes = (blocks / scale).astype(np.float32).astype(dtype).astype(np.float64)
    return np.moveaxis((codes * scale).reshape(v.shape), -1, axis)


WIDE = False


def mx_kscale(k):
    if not WIDE:
        return np.ones(k)
    levels = np.array([10, -10, 5, -5, 0])
    if k % 512:
        return np.exp2(np.random.permutation(np.resize(levels, k // 32))).repeat(32)
    a = np.empty((k // 512, 16))
    for p in range(k // 512):
        a[p, :8] = np.random.permutation(np.resize(levels, 8))
        for g in range(8):
            far = levels[np.abs(levels - a[p, g]) >= 10]
            a[p, g + 8] = far[np.random.randint(len(far))]
    return np.exp2(a.ravel()).repeat(32)


def f64(x):
    return np.asarray(x).astype(np.float64)


def striped(idx):
    return np.tile(np.asarray(idx).reshape(-1, 16).T, (8, 1)).astype(np.uint16)


def unstriped(offs):
    return offs[:16].T.reshape(-1).astype(np.int64)


E2M1 = np.array([0.0, 0.5, 1.0, 1.5, 2.0, 3.0, 4.0, 6.0, -0.0, -0.5, -1.0, -1.5, -2.0, -3.0, -4.0, -6.0])


def pack_weight(w, fmt):
    k, n = w.shape
    w = f64(np.asarray(w, np.float32).astype(ml_dtypes.bfloat16)).reshape(k // 32, 32, n)
    amax = np.abs(w).max(1)
    if fmt == "e4m3":
        byte = np.frexp(amax)[1] - 1 + 127 - 7
    else:
        mant, ex = np.frexp(amax / 6.0)
        byte = np.where(mant > 0.5, ex, ex - 1) + 127
    byte = np.clip(np.where(amax > 0, byte, 1), 1, 254)
    scaled = (w * np.exp2(127.0 - byte)[:, None, :]).reshape(k, n).astype(np.float32)
    by_word = np.ascontiguousarray(scaled.reshape(k // 512, 128, 4, n).transpose(0, 1, 3, 2))
    if fmt == "e4m3":
        words = by_word.astype(ml_dtypes.float8_e4m3fn).view(np.uint8)
    else:
        c = by_word.astype(ml_dtypes.float4_e2m1fn).view(np.uint8) & 0xF
        words = (c[..., 0::2] | (c[..., 1::2] << 4)).reshape(k // 512, 128, 2 * n)
    return np.ascontiguousarray(words), np.ascontiguousarray(byte.astype(np.uint8).reshape(k // 512, 16, n))


def unpack_weight(words, scales, fmt):
    g, _, n = scales.shape
    words = np.ascontiguousarray(words).reshape(g, 128, n, -1)
    if fmt == "e4m3":
        vals = words.view(ml_dtypes.float8_e4m3fn).astype(np.float64)
    else:
        nib = np.empty((g, 128, n, 4), np.uint8)
        nib[..., 0::2] = words & 0xF
        nib[..., 1::2] = words >> 4
        vals = E2M1[nib]
    vals = vals * np.repeat(np.exp2(scales.astype(np.float64) - 127.0), 8, axis=1)[..., None]
    return vals.transpose(0, 1, 3, 2).reshape(g * 512, n)


B, N, T, D, DV, NQ = 1, 512, 1024, 1024, 128, 256


def setup_inputs():
    n = np.random.standard_normal
    idx = np.random.permutation(T)[:B * N]
    s = mx_kscale(D)[:, None]
    u = np.ones(T)
    u[idx] = mx_kscale(B * N)
    r = np.random.uniform(0.5, 2.0, T)
    qp = [pack_weight(x, "e4m3") for x in n((B, D, NQ)) * s * (0.80 / np.sqrt(D))]
    k = n((D, T)) / s
    v = n((DV, T)) / (u * r)
    kp = pack_weight(k, "e4m3")
    return {
        "q_words": np.stack([x[0] for x in qp]),
        "q_scales": np.stack([x[1] for x in qp]),
        "k_words": kp[0],
        "k_scales": kp[1],
        "vT": v.astype(np.float32),
        "vs": np.tile(u * r, (128, 1)).astype(np.float32),
        "og": n((B, NQ, DV)).astype(np.float32),
        "offs": striped(idx),
    }


def reference(q_words, q_scales, k_words, k_scales, vT, vs, og, offs):
    idx = unstriped(offs)
    k = unpack_weight(k_words, k_scales, "e4m3")
    v = f64(vT)
    pick = lambda x: x[:, idx].reshape(x.shape[0], B, N).transpose(1, 0, 2)
    q = np.stack([unpack_weight(q_words[b], q_scales[b], "e4m3") for b in range(B)])
    score = q.transpose(0, 2, 1) @ pick(k)
    m = score.max(-1, keepdims=True)
    p = np.exp(score - m)
    total = p.sum(-1, keepdims=True)
    w = p * pick(f64(vs))[:, :1, :]
    y = mxq(w, 2, "e4m3") @ mxq(pick(v).transpose(0, 2, 1), 1, "e4m3")
    y = y / total
    y = y / (1.0 + np.exp(-f64(og)))
    return y

@@ -1,0 +1,149 @@
+from contextlib import ExitStack
+
+import concourse.mybir as mybir
+from concourse.masks import make_identity
+
+F32 = mybir.dt.float32
+BF16 = mybir.dt.bfloat16
+I32 = mybir.dt.int32
+U32 = mybir.dt.uint32
+U16 = mybir.dt.uint16
+U8 = mybir.dt.uint8
+FP8X4 = mybir.dt.float8_e4m3fn_x4
+ACT = mybir.ActivationFunctionType
+ALU = mybir.AluOpType
+AX = mybir.AxisListType
+
+P = 128
+PACK = 4
+SLOTS = 512
+POOL = 1024
+QUERIES = 256
+DV = 128
+PASSES = 2
+Q_TILES = QUERIES // P
+FLOPS = 2 * QUERIES * SLOTS * (PASSES * P * PACK + DV)
+
+
+def tile_attend_soft_gate_topkq256n512t1024_kernel(tc, q_words, q_scales, k_words, k_scales, vT, vs, og, offs, out):
+    nc = tc.nc
+    with ExitStack() as ctx:
+        sb = ctx.enter_context(tc.tile_pool(name="sb", bufs=1))
+        ps = ctx.enter_context(tc.psum_pool(name="ps", bufs=1))
+
+        offsets = sb.tile([P, SLOTS // 16], U16, name="offsets")
+        k_pool = [sb.tile([P, POOL], U32, name=f"k_pool{o}", align_bytes=64) for o in range(PASSES)]
+        ks_pool = sb.tile([P, POOL], U8, name="ks_pool", align_bytes=64)
+        vs_pool = sb.tile([P, POOL], F32, name="vs_pool", align_bytes=64)
+        v_pool = sb.tile([P, POOL], F32, name="v_pool", align_bytes=64)
+        q_codes = sb.tile([P, PASSES, QUERIES], U32, name="q_codes", align_bytes=64)
+        q_planes = sb.tile([P, QUERIES], U8, name="q_planes", align_bytes=64)
+        gate_in = sb.tile([P, Q_TILES, DV], F32, name="gate_in", align_bytes=64)
+        ident = sb.tile([P, P], F32, name="ident", align_bytes=64)
+
+        nc.gpsimd.memset(ks_pool[:].bitcast(I32), 0)
+        nc.gpsimd.memset(q_planes[:].bitcast(I32), 0)
+        nc.vector.memset(vs_pool[0:96, :], 0.0)
+        make_identity(nc, ident[:])
+
+        nc.sync.dma_start(offsets[:], offs)
+        nc.sync.dma_start(vs_pool[96:128, :], vs[96:128, :])
+        for quad in range(4):
+            nc.sync.dma_start(ks_pool[32 * quad : 32 * quad + 8, :].bitcast(I32), k_scales[:, 4 * quad : 4 * quad + 4, :].bitcast(I32))
+        nc.sync.dma_start(k_pool[0][:].bitcast(I32), k_words[0].rearrange("p n t -> p (n t)").bitcast(I32))
+        nc.sync.dma_start(q_codes[:].bitcast(I32), q_words[0].rearrange("o p n t -> p o (n t)").bitcast(I32))
+        for quad in range(4):
+            nc.sync.dma_start(q_planes[32 * quad : 32 * quad + 8, :].bitcast(I32), q_scales[0][:, 4 * quad : 4 * quad + 4, :].bitcast(I32))
+        nc.sync.dma_start(k_pool[1][:].bitcast(I32), k_words[1].rearrange("p n t -> p (n t)").bitcast(I32))
+        nc.sync.dma_start(gate_in[:], og[0].rearrange("(j p) e -> p j e", p=P))
+        nc.sync.dma_start(v_pool[:], vT)
+
+        vs_row = sb.tile([P, SLOTS], F32, name="vs_row", align_bytes=64)
+        nc.vector.tensor_copy(vs_row[:], vs_pool[:].indirect(offsets[:]))
+        k_planes = sb.tile([P, SLOTS], U8, name="k_planes", align_bytes=64)
+        nc.vector.tensor_copy(k_planes[:], ks_pool[:].indirect(offsets[:]))
+        k_codes = [sb.tile([P, SLOTS], U32, name=f"k_codes{o}", tag=f"gathered{o}", align_bytes=64) for o in range(PASSES)]
+        for o in range(PASSES):
+            nc.vector.tensor_copy(k_codes[o][:], k_pool[o][:].indirect(offsets[:]))
+
+        vs_turned = ps.tile([P, PACK, P], F32, name="vs_turned")
+        for t in range(PACK):
+            nc.tensor.transpose(vs_turned[:, t, :], vs_row[:, t::PACK], ident[:])
+        vs_cols = sb.tile([P, PACK], F32, name="vs_cols", align_bytes=64)
+        nc.scalar.copy(vs_cols[:], vs_turned[:, :, 96])
+
+        gate_tanh = sb.tile([P, Q_TILES, DV], F32, name="gate_tanh", align_bytes=64)
+        nc.scalar.activation(gate_tanh[:], gate_in[:], ACT.Tanh, scale=0.5)
+        gate = sb.tile([P, Q_TILES, DV], F32, name="gate", align_bytes=64)
+        nc.scalar.activation(gate[:], gate_tanh[:], ACT.Copy, scale=0.5, bias=0.5)
+
+        scores = [ps.tile([P, SLOTS], F32, name=f"scores{j}", tag=f"scores{j}") for j in range(Q_TILES)]
+        for o in range(PASSES):
+            for j in range(Q_TILES):
+                rows = slice(j * P, (j + 1) * P)
+                nc.tensor.matmul_mx(
+                    out=scores[j][:],
+                    lhsT=q_codes[:, o, rows].bitcast(FP8X4),
+                    lhsT_scale=q_planes[4 * o :, rows],
+                    rhs=k_codes[o][:].bitcast(FP8X4),
+                    rhs_scale=k_planes[4 * o :, :],
+                    start=(o == 0),
+                    stop=(o == PASSES - 1),
+                )
+
+        probs, totals = [], []
+        for j in range(Q_TILES):
+            neg_max = sb.tile([P, 1], F32, name=f"neg_max{j}")
+            nc.vector.tensor_reduce(neg_max[:], scores[j][:], AX.X, ALU.max, negate=True)
+            probs.append(sb.tile([P, PACK, P], F32, name=f"probs{j}", align_bytes=64))
+            totals.append(sb.tile([P, 1], F32, name=f"total{j}"))
+            nc.scalar.activation(probs[j][:], scores[j][:].rearrange("p (s t) -> p t s", t=PACK), ACT.Exp, bias=neg_max[:], scale=1.0, accum_out=totals[j][:])
+
+        v_rows = sb.tile([P, SLOTS], BF16, name="v_rows", tag="gathered1", align_bytes=64)
+        nc.vector.tensor_copy(v_rows[:], v_pool[:].indirect(offsets[:]))
+
+        p_turned = [ps.tile([P, PACK, P], F32, name=f"p_turned{j}") for j in range(Q_TILES)]
+        for j in range(Q_TILES):
+            for t in range(PACK):
+                nc.tensor.transpose(p_turned[j][:, t, :], probs[j][:, t, :], ident[:])
+
+        v_turned = ps.tile([P, 2, P], F32, name="v_turned", tag="scores1")
+        v_pairs = v_rows[:].bitcast(F32)
+        for u in range(2):
+            nc.tensor.transpose(v_turned[:, u, :], v_pairs[:, u::2], ident[:])
+        v_grouped = sb.tile([P, DV * PACK], BF16, name="v_grouped", align_bytes=64)
+        nc.scalar.copy(v_grouped[:].bitcast(F32).rearrange("p (e u) -> p e u", u=2), v_turned[:].rearrange("p u e -> p e u"))
+
+        w_grouped, w_codes, w_planes, inv_totals = [], [], [], []
+        for j in range(Q_TILES):
+            w_grouped.append(sb.tile([P, P, PACK], BF16, name=f"w_grouped{j}", align_bytes=64))
+            nc.vector.tensor_tensor(
+                w_grouped[j][:],
+                p_turned[j][:].rearrange("p t q -> p q t"),
+                vs_cols[:].unsqueeze(1).to_broadcast([P, P, PACK]),
+                ALU.mult,
+            )
+        for j in range(Q_TILES):
+            w_codes.append(sb.tile([P, P], U32, name=f"w_codes{j}", align_bytes=64))
+            w_planes.append(sb.tile([P, P], U8, name=f"w_plane{j}", align_bytes=64))
+            nc.vector.quantize_mx(out=w_codes[j][:].bitcast(FP8X4), scales=w_planes[j][:], in_=w_grouped[j][:].rearrange("p q t -> p (q t)"))
+            inv_totals.append(sb.tile([P, 1], F32, name=f"inv_total{j}"))
+            nc.vector.reciprocal(inv_totals[j][:], totals[j][:])
+        v_codes = sb.tile([P, DV], U32, name="v_codes", align_bytes=64)
+        v_plane = sb.tile([P, DV], U8, name="v_plane", align_bytes=64)
+        nc.vector.quantize_mx(out=v_codes[:].bitcast(FP8X4), scales=v_plane[:], in_=v_grouped[:])
+
+        for j in range(Q_TILES):
+            sums = ps.tile([P, DV], F32, name=f"sums{j}")
+            nc.tensor.matmul_mx(
+                out=sums[:],
+                lhsT=w_codes[j][:].bitcast(FP8X4),
+                lhsT_scale=w_planes[j][:],
+                rhs=v_codes[:].bitcast(FP8X4),
+                rhs_scale=v_plane[:],
+                start=True,
+                stop=True,
+            )
+            result = sb.tile([P, DV], F32, name=f"result{j}", align_bytes=64)
+            nc.vector.scalar_tensor_tensor(result[:], sums[:], inv_totals[j][:], gate[:, j, :], ALU.mult, ALU.mult)
+            nc.sync.dma_start(out[0][j * P : (j + 1) * P, :], result[:])

@@ -43,7 +43,7 @@ def tile_attend_soft_gate_topkq256n512t1024_kernel(tc, q_words, q_scales, k_word
 
         nc.gpsimd.memset(ks_pool[:].bitcast(I32), 0)
         nc.gpsimd.memset(q_planes[:].bitcast(I32), 0)
-        nc.vector.memset(vs_pool[0:96, :], 0.0)
+        nc.gpsimd.memset(vs_pool[0:96, :], 0.0)
         make_identity(nc, ident[:])
 
         nc.sync.dma_start(offsets[:], offs)
@@ -51,10 +51,10 @@ def tile_attend_soft_gate_topkq256n512t1024_kernel(tc, q_words, q_scales, k_word
         for quad in range(4):
             nc.sync.dma_start(ks_pool[32 * quad : 32 * quad + 8, :].bitcast(I32), k_scales[:, 4 * quad : 4 * quad + 4, :].bitcast(I32))
         nc.sync.dma_start(k_pool[0][:].bitcast(I32), k_words[0].rearrange("p n t -> p (n t)").bitcast(I32))
+        nc.sync.dma_start(k_pool[1][:].bitcast(I32), k_words[1].rearrange("p n t -> p (n t)").bitcast(I32))
         nc.sync.dma_start(q_codes[:].bitcast(I32), q_words[0].rearrange("o p n t -> p o (n t)").bitcast(I32))
         for quad in range(4):
             nc.sync.dma_start(q_planes[32 * quad : 32 * quad + 8, :].bitcast(I32), q_scales[0][:, 4 * quad : 4 * quad + 4, :].bitcast(I32))
-        nc.sync.dma_start(k_pool[1][:].bitcast(I32), k_words[1].rearrange("p n t -> p (n t)").bitcast(I32))
         nc.sync.dma_start(gate_in[:], og[0].rearrange("(j p) e -> p j e", p=P))
         nc.sync.dma_start(v_pool[:], vT)
 
@@ -91,30 +91,27 @@ def tile_attend_soft_gate_topkq256n512t1024_kernel(tc, q_words, q_scales, k_word
                     stop=(o == PASSES - 1),
                 )
 
-        probs, totals = [], []
+        sub_totals = sb.tile([P, Q_TILES, 2], F32, name="sub_totals")
+        p_turned = [ps.tile([P, PACK, P], F32, name=f"p_turned{j}") for j in range(Q_TILES)]
         for j in range(Q_TILES):
             neg_max = sb.tile([P, 1], F32, name=f"neg_max{j}")
             nc.vector.tensor_reduce(neg_max[:], scores[j][:], AX.X, ALU.max, negate=True)
-            probs.append(sb.tile([P, PACK, P], F32, name=f"probs{j}", align_bytes=64))
-            totals.append(sb.tile([P, 1], F32, name=f"total{j}"))
-            nc.scalar.activation(probs[j][:], scores[j][:].rearrange("p (s t) -> p t s", t=PACK), ACT.Exp, bias=neg_max[:], scale=1.0, accum_out=totals[j][:])
+            dealt = scores[j][:].rearrange("p (s t) -> p t s", t=PACK)
+            for u in range(2):
+                probs = sb.tile([P, 2, P], F32, name=f"probs{j}{u}", align_bytes=64)
+                nc.scalar.activation(probs[:], dealt[:, 2 * u : 2 * u + 2, :], ACT.Exp, bias=neg_max[:], scale=1.0, accum_out=sub_totals[:, j, u : u + 1])
+                for e in range(2):
+                    nc.tensor.transpose(p_turned[j][:, 2 * u + e, :], probs[:, e, :], ident[:])
 
         v_rows = sb.tile([P, SLOTS], BF16, name="v_rows", tag="gathered1", align_bytes=64)
         nc.vector.tensor_copy(v_rows[:], v_pool[:].indirect(offsets[:]))
-
-        p_turned = [ps.tile([P, PACK, P], F32, name=f"p_turned{j}") for j in range(Q_TILES)]
-        for j in range(Q_TILES):
-            for t in range(PACK):
-                nc.tensor.transpose(p_turned[j][:, t, :], probs[j][:, t, :], ident[:])
-
         v_turned = ps.tile([P, 2, P], F32, name="v_turned", tag="scores1")
         v_pairs = v_rows[:].bitcast(F32)
         for u in range(2):
             nc.tensor.transpose(v_turned[:, u, :], v_pairs[:, u::2], ident[:])
         v_grouped = sb.tile([P, DV * PACK], BF16, name="v_grouped", align_bytes=64)
         nc.scalar.copy(v_grouped[:].bitcast(F32).rearrange("p (e u) -> p e u", u=2), v_turned[:].rearrange("p u e -> p e u"))
-
-        w_grouped, w_codes, w_planes, inv_totals = [], [], [], []
+        w_grouped, w_codes, w_planes = [], [], []
         for j in range(Q_TILES):
             w_grouped.append(sb.tile([P, P, PACK], BF16, name=f"w_grouped{j}", align_bytes=64))
             nc.vector.tensor_tensor(
@@ -127,8 +124,11 @@ def tile_attend_soft_gate_topkq256n512t1024_kernel(tc, q_words, q_scales, k_word
             w_codes.append(sb.tile([P, P], U32, name=f"w_codes{j}", align_bytes=64))
             w_planes.append(sb.tile([P, P], U8, name=f"w_plane{j}", align_bytes=64))
             nc.vector.quantize_mx(out=w_codes[j][:].bitcast(FP8X4), scales=w_planes[j][:], in_=w_grouped[j][:].rearrange("p q t -> p (q t)"))
-            inv_totals.append(sb.tile([P, 1], F32, name=f"inv_total{j}"))
-            nc.vector.reciprocal(inv_totals[j][:], totals[j][:])
+        totals = sb.tile([P, Q_TILES], F32, name="totals")
+        nc.vector.tensor_reduce(totals[:], sub_totals[:], AX.X, ALU.add)
+        inv_totals = sb.tile([P, Q_TILES], F32, name="inv_totals")
+        nc.vector.reciprocal(inv_totals[:], totals[:])
+
         v_codes = sb.tile([P, DV], U32, name="v_codes", align_bytes=64)
         v_plane = sb.tile([P, DV], U8, name="v_plane", align_bytes=64)
         nc.vector.quantize_mx(out=v_codes[:].bitcast(FP8X4), scales=v_plane[:], in_=v_grouped[:])
@@ -145,5 +145,5 @@ def tile_attend_soft_gate_topkq256n512t1024_kernel(tc, q_words, q_scales, k_word
                 stop=True,
             )
             result = sb.tile([P, DV], F32, name=f"result{j}", align_bytes=64)
-            nc.vector.scalar_tensor_tensor(result[:], sums[:], inv_totals[j][:], gate[:, j, :], ALU.mult, ALU.mult)
+            nc.vector.scalar_tensor_tensor(result[:], sums[:], inv_totals[:, j : j + 1], gate[:, j, :], ALU.mult, ALU.mult)
             nc.sync.dma_start(out[0][j * P : (j + 1) * P, :], result[:])

from contextlib import ExitStack

import concourse.mybir as mybir
from concourse.masks import make_identity

F32 = mybir.dt.float32
BF16 = mybir.dt.bfloat16
I32 = mybir.dt.int32
U32 = mybir.dt.uint32
U16 = mybir.dt.uint16
U8 = mybir.dt.uint8
FP8X4 = mybir.dt.float8_e4m3fn_x4
ACT = mybir.ActivationFunctionType
ALU = mybir.AluOpType
AX = mybir.AxisListType

P = 128
PACK = 4
SLOTS = 512
POOL = 1024
QUERIES = 256
DV = 128
PASSES = 2
Q_TILES = QUERIES // P
FLOPS = 2 * QUERIES * SLOTS * (PASSES * P * PACK + DV)


def tile_attend_soft_gate_topkq256n512t1024_kernel(tc, q_words, q_scales, k_words, k_scales, vT, vs, og, offs, out):
    nc = tc.nc
    with ExitStack() as ctx:
        sb = ctx.enter_context(tc.tile_pool(name="sb", bufs=1))
        ps = ctx.enter_context(tc.psum_pool(name="ps", bufs=1))

        offsets = sb.tile([P, SLOTS // 16], U16, name="offsets")
        k_pool = [sb.tile([P, POOL], U32, name=f"k_pool{o}", align_bytes=64) for o in range(PASSES)]
        ks_pool = sb.tile([P, POOL], U8, name="ks_pool", align_bytes=64)
        vs_pool = sb.tile([P, POOL], F32, name="vs_pool", align_bytes=64)
        v_pool = sb.tile([P, POOL], F32, name="v_pool", align_bytes=64)
        q_codes = sb.tile([P, PASSES, QUERIES], U32, name="q_codes", align_bytes=64)
        q_planes = sb.tile([P, QUERIES], U8, name="q_planes", align_bytes=64)
        gate_in = sb.tile([P, Q_TILES, DV], F32, name="gate_in", align_bytes=64)
        ident = sb.tile([P, P], F32, name="ident", align_bytes=64)

        nc.gpsimd.memset(ks_pool[:].bitcast(I32), 0)
        nc.gpsimd.memset(q_planes[:].bitcast(I32), 0)
        nc.gpsimd.memset(vs_pool[0:96, :], 0.0)
        make_identity(nc, ident[:])

        nc.sync.dma_start(offsets[:], offs)
        nc.sync.dma_start(vs_pool[96:128, :], vs[96:128, :])
        for quad in range(4):
            nc.sync.dma_start(ks_pool[32 * quad : 32 * quad + 8, :].bitcast(I32), k_scales[:, 4 * quad : 4 * quad + 4, :].bitcast(I32))
        nc.sync.dma_start(k_pool[0][:].bitcast(I32), k_words[0].rearrange("p n t -> p (n t)").bitcast(I32))
        nc.sync.dma_start(k_pool[1][:].bitcast(I32), k_words[1].rearrange("p n t -> p (n t)").bitcast(I32))
        nc.sync.dma_start(q_codes[:].bitcast(I32), q_words[0].rearrange("o p n t -> p o (n t)").bitcast(I32))
        for quad in range(4):
            nc.sync.dma_start(q_planes[32 * quad : 32 * quad + 8, :].bitcast(I32), q_scales[0][:, 4 * quad : 4 * quad + 4, :].bitcast(I32))
        nc.sync.dma_start(gate_in[:], og[0].rearrange("(j p) e -> p j e", p=P))
        nc.sync.dma_start(v_pool[:], vT)

        vs_row = sb.tile([P, SLOTS], F32, name="vs_row", align_bytes=64)
        nc.vector.tensor_copy(vs_row[:], vs_pool[:].indirect(offsets[:]))
        k_planes = sb.tile([P, SLOTS], U8, name="k_planes", align_bytes=64)
        nc.vector.tensor_copy(k_planes[:], ks_pool[:].indirect(offsets[:]))
        k_codes = [sb.tile([P, SLOTS], U32, name=f"k_codes{o}", tag=f"gathered{o}", align_bytes=64) for o in range(PASSES)]
        for o in range(PASSES):
            nc.vector.tensor_copy(k_codes[o][:], k_pool[o][:].indirect(offsets[:]))

        vs_turned = ps.tile([P, PACK, P], F32, name="vs_turned")
        for t in range(PACK):
            nc.tensor.transpose(vs_turned[:, t, :], vs_row[:, t::PACK], ident[:])
        vs_cols = sb.tile([P, PACK], F32, name="vs_cols", align_bytes=64)
        nc.scalar.copy(vs_cols[:], vs_turned[:, :, 96])

        gate_tanh = sb.tile([P, Q_TILES, DV], F32, name="gate_tanh", align_bytes=64)
        nc.scalar.activation(gate_tanh[:], gate_in[:], ACT.Tanh, scale=0.5)
        gate = sb.tile([P, Q_TILES, DV], F32, name="gate", align_bytes=64)
        nc.scalar.activation(gate[:], gate_tanh[:], ACT.Copy, scale=0.5, bias=0.5)

        scores = [ps.tile([P, SLOTS], F32, name=f"scores{j}", tag=f"scores{j}") for j in range(Q_TILES)]
        for o in range(PASSES):
            for j in range(Q_TILES):
                rows = slice(j * P, (j + 1) * P)
                nc.tensor.matmul_mx(
                    out=scores[j][:],
                    lhsT=q_codes[:, o, rows].bitcast(FP8X4),
                    lhsT_scale=q_planes[4 * o :, rows],
                    rhs=k_codes[o][:].bitcast(FP8X4),
                    rhs_scale=k_planes[4 * o :, :],
                    start=(o == 0),
                    stop=(o == PASSES - 1),
                )

        sub_totals = sb.tile([P, Q_TILES, 2], F32, name="sub_totals")
        p_turned = [ps.tile([P, PACK, P], F32, name=f"p_turned{j}") for j in range(Q_TILES)]
        for j in range(Q_TILES):
            neg_max = sb.tile([P, 1], F32, name=f"neg_max{j}")
            nc.vector.tensor_reduce(neg_max[:], scores[j][:], AX.X, ALU.max, negate=True)
            dealt = scores[j][:].rearrange("p (s t) -> p t s", t=PACK)
            for u in range(2):
                probs = sb.tile([P, 2, P], F32, name=f"probs{j}{u}", align_bytes=64)
                nc.scalar.activation(probs[:], dealt[:, 2 * u : 2 * u + 2, :], ACT.Exp, bias=neg_max[:], scale=1.0, accum_out=sub_totals[:, j, u : u + 1])
                for e in range(2):
                    nc.tensor.transpose(p_turned[j][:, 2 * u + e, :], probs[:, e, :], ident[:])

        v_rows = sb.tile([P, SLOTS], BF16, name="v_rows", tag="gathered1", align_bytes=64)
        nc.vector.tensor_copy(v_rows[:], v_pool[:].indirect(offsets[:]))
        v_turned = ps.tile([P, 2, P], F32, name="v_turned", tag="scores1")
        v_pairs = v_rows[:].bitcast(F32)
        for u in range(2):
            nc.tensor.transpose(v_turned[:, u, :], v_pairs[:, u::2], ident[:])
        v_grouped = sb.tile([P, DV * PACK], BF16, name="v_grouped", align_bytes=64)
        nc.scalar.copy(v_grouped[:].bitcast(F32).rearrange("p (e u) -> p e u", u=2), v_turned[:].rearrange("p u e -> p e u"))
        w_grouped, w_codes, w_planes = [], [], []
        for j in range(Q_TILES):
            w_grouped.append(sb.tile([P, P, PACK], BF16, name=f"w_grouped{j}", align_bytes=64))
            nc.vector.tensor_tensor(
                w_grouped[j][:],
                p_turned[j][:].rearrange("p t q -> p q t"),
                vs_cols[:].unsqueeze(1).to_broadcast([P, P, PACK]),
                ALU.mult,
            )
        for j in range(Q_TILES):
            w_codes.append(sb.tile([P, P], U32, name=f"w_codes{j}", align_bytes=64))
            w_planes.append(sb.tile([P, P], U8, name=f"w_plane{j}", align_bytes=64))
            nc.vector.quantize_mx(out=w_codes[j][:].bitcast(FP8X4), scales=w_planes[j][:], in_=w_grouped[j][:].rearrange("p q t -> p (q t)"))
        totals = sb.tile([P, Q_TILES], F32, name="totals")
        nc.vector.tensor_reduce(totals[:], sub_totals[:], AX.X, ALU.add)
        inv_totals = sb.tile([P, Q_TILES], F32, name="inv_totals")
        nc.vector.reciprocal(inv_totals[:], totals[:])

        v_codes = sb.tile([P, DV], U32, name="v_codes", align_bytes=64)
        v_plane = sb.tile([P, DV], U8, name="v_plane", align_bytes=64)
        nc.vector.quantize_mx(out=v_codes[:].bitcast(FP8X4), scales=v_plane[:], in_=v_grouped[:])

        for j in range(Q_TILES):
            sums = ps.tile([P, DV], F32, name=f"sums{j}")
            nc.tensor.matmul_mx(
                out=sums[:],
                lhsT=w_codes[j][:].bitcast(FP8X4),
                lhsT_scale=w_planes[j][:],
                rhs=v_codes[:].bitcast(FP8X4),
                rhs_scale=v_plane[:],
                start=True,
                stop=True,
            )
            result = sb.tile([P, DV], F32, name=f"result{j}", align_bytes=64)
            nc.vector.scalar_tensor_tensor(result[:], sums[:], inv_totals[:, j : j + 1], gate[:, j, :], ALU.mult, ALU.mult)
            nc.sync.dma_start(out[0][j * P : (j + 1) * P, :], result[:])
